import numpy as np
import ml_dtypes

BF16 = ml_dtypes.bfloat16


def bf(x):
    return np.asarray(x, np.float32).astype(BF16)


def f32(x):
    return np.asarray(x, np.float32)


def f64(x):
    return np.asarray(x).astype(np.float64)


def striped(idx):
    return np.tile(idx.reshape(-1, 16).T, (8, 1))


S, K, M, N = 4096, 512, 128, 1536


def sigmoid(v):
    return 1.0 / (1.0 + np.exp(-v))


def setup_inputs():
    return {"table": bf(np.random.standard_normal((K, S))), "w": bf(np.random.standard_normal((K, M)) / np.sqrt(K)), "b": f32(0.5 * np.random.standard_normal((M, 1))), "offs": striped(np.random.permutation(S)[:N])}


def reference(table, w, b, offs):
    idx = offs[:16].T.reshape(-1)
    x = f64(table)[:, idx]
    y = f64(w).T @ x
    return (y + f64(b)) * sigmoid(y + f64(b))

@@ -1,0 +1,48 @@
+import concourse.mybir as mybir
+
+BF16, F32, U16 = mybir.dt.bfloat16, mybir.dt.float32, mybir.dt.uint16
+SILU = mybir.ActivationFunctionType.Silu
+
+P = 128
+K, S, M, N = 512, 4096, 128, 1536
+K_BLOCKS = K // P
+PIECE = 512
+PIECES = N // PIECE
+PIECE_COLS = PIECE // 16
+
+FLOPS = 2 * K * M * N
+
+
+def tile_gather_matmul_kernel(tc, table, w, b, offs, out):
+    nc = tc.nc
+    with (
+        tc.tile_pool(name="held", bufs=1) as held,
+        tc.psum_pool(name="psum", bufs=1) as psum,
+    ):
+        offsets = held.tile([P, N // 16], U16, name="offsets")
+        nc.sync.dma_start(offsets[:], offs)
+
+        blocks = []
+        for kb in range(K_BLOCKS):
+            block = held.tile([P, S], BF16, name=f"block{kb}")
+            nc.sync.dma_start(block[:], table[kb * P : (kb + 1) * P, :])
+            blocks.append(block)
+
+        weights = held.tile([P, K_BLOCKS, M], BF16, name="weights")
+        nc.scalar.dma_start(weights[:], w.rearrange("(kb p) m -> p kb m", p=P))
+        bias = held.tile([P, 1], F32, name="bias")
+        nc.scalar.dma_start(bias[:], b)
+
+        banks = [psum.tile([P, PIECE], F32, name=f"bank{j}") for j in range(PIECES)]
+        for kb in range(K_BLOCKS):
+            for j in range(PIECES):
+                picked = blocks[kb][:].indirect(offsets[:, j * PIECE_COLS : (j + 1) * PIECE_COLS])
+                nc.tensor.matmul(
+                    banks[j][:], weights[:, kb, :], picked,
+                    start=(kb == 0), stop=(kb == K_BLOCKS - 1),
+                )
+
+        for j in range(PIECES):
+            result = held.tile([P, PIECE], F32, name=f"result{j}")
+            nc.scalar.activation(result[:], banks[j][:], SILU, bias=bias[:, 0:1])
+            nc.sync.dma_start(out[:, j * PIECE : (j + 1) * PIECE], result[:])

@@ -10,6 +10,8 @@ PIECE = 512
 PIECES = N // PIECE
 PIECE_COLS = PIECE // 16
 
+WARM_MATMULS = 8
+
 FLOPS = 2 * K * M * N
 
 
@@ -19,17 +21,24 @@ def tile_gather_matmul_kernel(tc, table, w, b, offs, out):
         tc.tile_pool(name="held", bufs=1) as held,
         tc.psum_pool(name="psum", bufs=1) as psum,
     ):
+        zeros = held.tile([P, PIECE], BF16, name="zeros")
+        nc.vector.memset(zeros[:], 0.0)
+        unread = psum.tile([P, PIECE], F32, name="unread")
+        for _ in range(WARM_MATMULS):
+            nc.tensor.matmul(unread[:], zeros[:, 0:P], zeros[:], start=True, stop=True)
+
         offsets = held.tile([P, N // 16], U16, name="offsets")
         nc.sync.dma_start(offsets[:], offs)
 
+        table_blocks = table.rearrange("(p kb) s -> kb p s", kb=K_BLOCKS)
         blocks = []
         for kb in range(K_BLOCKS):
             block = held.tile([P, S], BF16, name=f"block{kb}")
-            nc.sync.dma_start(block[:], table[kb * P : (kb + 1) * P, :])
+            nc.sync.dma_start(block[:], table_blocks[kb])
             blocks.append(block)
 
         weights = held.tile([P, K_BLOCKS, M], BF16, name="weights")
-        nc.scalar.dma_start(weights[:], w.rearrange("(kb p) m -> p kb m", p=P))
+        nc.scalar.dma_start(weights[:], w.rearrange("(p kb) m -> p kb m", kb=K_BLOCKS))
         bias = held.tile([P, 1], F32, name="bias")
         nc.scalar.dma_start(bias[:], b)
 

@@ -10,6 +10,8 @@ PIECE = 512
 PIECES = N // PIECE
 PIECE_COLS = PIECE // 16
 
+DMA_ALIGN = 256
+
 WARM_MATMULS = 8
 
 FLOPS = 2 * K * M * N
@@ -33,11 +35,11 @@ def tile_gather_matmul_kernel(tc, table, w, b, offs, out):
         table_blocks = table.rearrange("(p kb) s -> kb p s", kb=K_BLOCKS)
         blocks = []
         for kb in range(K_BLOCKS):
-            block = held.tile([P, S], BF16, name=f"block{kb}")
+            block = held.tile([P, S], BF16, name=f"block{kb}", align_bytes=DMA_ALIGN)
             nc.sync.dma_start(block[:], table_blocks[kb])
             blocks.append(block)
 
-        weights = held.tile([P, K_BLOCKS, M], BF16, name="weights")
+        weights = held.tile([P, K_BLOCKS, M], BF16, name="weights", align_bytes=DMA_ALIGN)
         nc.scalar.dma_start(weights[:], w.rearrange("(p kb) m -> p kb m", kb=K_BLOCKS))
         bias = held.tile([P, 1], F32, name="bias")
         nc.scalar.dma_start(bias[:], b)
@@ -52,6 +54,6 @@ def tile_gather_matmul_kernel(tc, table, w, b, offs, out):
                 )
 
         for j in range(PIECES):
-            result = held.tile([P, PIECE], F32, name=f"result{j}")
+            result = held.tile([P, PIECE], F32, name=f"result{j}", align_bytes=DMA_ALIGN)
             nc.scalar.activation(result[:], banks[j][:], SILU, bias=bias[:, 0:1])
             nc.sync.dma_start(out[:, j * PIECE : (j + 1) * PIECE], result[:])

@@ -12,8 +12,6 @@ PIECE_COLS = PIECE // 16
 
 DMA_ALIGN = 256
 
-WARM_MATMULS = 8
-
 FLOPS = 2 * K * M * N
 
 
@@ -23,12 +21,6 @@ def tile_gather_matmul_kernel(tc, table, w, b, offs, out):
         tc.tile_pool(name="held", bufs=1) as held,
         tc.psum_pool(name="psum", bufs=1) as psum,
     ):
-        zeros = held.tile([P, PIECE], BF16, name="zeros")
-        nc.vector.memset(zeros[:], 0.0)
-        unread = psum.tile([P, PIECE], F32, name="unread")
-        for _ in range(WARM_MATMULS):
-            nc.tensor.matmul(unread[:], zeros[:, 0:P], zeros[:], start=True, stop=True)
-
         offsets = held.tile([P, N // 16], U16, name="offsets")
         nc.sync.dma_start(offsets[:], offs)
 

@@ -12,6 +12,8 @@ PIECE_COLS = PIECE // 16
 
 DMA_ALIGN = 256
 
+BLOCK_SPACING = 64 * 1024
+
 FLOPS = 2 * K * M * N
 
 
@@ -19,6 +21,7 @@ def tile_gather_matmul_kernel(tc, table, w, b, offs, out):
     nc = tc.nc
     with (
         tc.tile_pool(name="held", bufs=1) as held,
+        tc.tile_pool(name="windows", bufs=1) as windows,
         tc.psum_pool(name="psum", bufs=1) as psum,
     ):
         offsets = held.tile([P, N // 16], U16, name="offsets")
@@ -27,7 +30,9 @@ def tile_gather_matmul_kernel(tc, table, w, b, offs, out):
         table_blocks = table.rearrange("(p kb) s -> kb p s", kb=K_BLOCKS)
         blocks = []
         for kb in range(K_BLOCKS):
-            block = held.tile([P, S], BF16, name=f"block{kb}", align_bytes=DMA_ALIGN)
+            block = windows.tile(
+                [P, S], BF16, name=f"block{kb}", offset=kb * BLOCK_SPACING, align_bytes=DMA_ALIGN
+            )
             nc.sync.dma_start(block[:], table_blocks[kb])
             blocks.append(block)
 

import concourse.mybir as mybir

BF16, F32, U16 = mybir.dt.bfloat16, mybir.dt.float32, mybir.dt.uint16
SILU = mybir.ActivationFunctionType.Silu

P = 128
K, S, M, N = 512, 4096, 128, 1536
K_BLOCKS = K // P
PIECE = 512
PIECES = N // PIECE
PIECE_COLS = PIECE // 16

DMA_ALIGN = 256

BLOCK_SPACING = 64 * 1024

FLOPS = 2 * K * M * N


def tile_gather_matmul_kernel(tc, table, w, b, offs, out):
    nc = tc.nc
    with (
        tc.tile_pool(name="held", bufs=1) as held,
        tc.tile_pool(name="windows", bufs=1) as windows,
        tc.psum_pool(name="psum", bufs=1) as psum,
    ):
        offsets = held.tile([P, N // 16], U16, name="offsets")
        nc.sync.dma_start(offsets[:], offs)

        table_blocks = table.rearrange("(p kb) s -> kb p s", kb=K_BLOCKS)
        blocks = []
        for kb in range(K_BLOCKS):
            block = windows.tile(
                [P, S], BF16, name=f"block{kb}", offset=kb * BLOCK_SPACING, align_bytes=DMA_ALIGN
            )
            nc.sync.dma_start(block[:], table_blocks[kb])
            blocks.append(block)

        weights = held.tile([P, K_BLOCKS, M], BF16, name="weights", align_bytes=DMA_ALIGN)
        nc.scalar.dma_start(weights[:], w.rearrange("(p kb) m -> p kb m", kb=K_BLOCKS))
        bias = held.tile([P, 1], F32, name="bias")
        nc.scalar.dma_start(bias[:], b)

        banks = [psum.tile([P, PIECE], F32, name=f"bank{j}") for j in range(PIECES)]
        for kb in range(K_BLOCKS):
            for j in range(PIECES):
                picked = blocks[kb][:].indirect(offsets[:, j * PIECE_COLS : (j + 1) * PIECE_COLS])
                nc.tensor.matmul(
                    banks[j][:], weights[:, kb, :], picked,
                    start=(kb == 0), stop=(kb == K_BLOCKS - 1),
                )

        for j in range(PIECES):
            result = held.tile([P, PIECE], F32, name=f"result{j}", align_bytes=DMA_ALIGN)
            nc.scalar.activation(result[:], banks[j][:], SILU, bias=bias[:, 0:1])
            nc.sync.dma_start(out[:, j * PIECE : (j + 1) * PIECE], result[:])
